import numpy as np
import ml_dtypes


def mxq(x, axis, fmt="e4m3"):
    dtype, down = {"e4m3": (ml_dtypes.float8_e4m3fn, 7), "e5m2": (ml_dtypes.float8_e5m2, 14)}[fmt]
    v = np.moveaxis(np.asarray(x, np.float32).astype(ml_dtypes.bfloat16).astype(np.float64), axis, -1)
    blocks = v.reshape(v.shape[:-1] + (-1, 32))
    amax = np.abs(blocks).max(-1, keepdims=True)
    byte = np.maximum(np.where(amax > 0, np.frexp(amax)[1] - 1 + 127, 0) - down, 1)
    scale = np.exp2(byte - 127.0)
    codes = (blocks / scale).astype(np.float32).astype(dtype).astype(np.float64)
    return np.moveaxis((codes * scale).reshape(v.shape), -1, axis)


WIDE = False


def mx_kscale(k):
    if not WIDE:
        return np.ones(k)
    levels = np.array([10, -10, 5, -5, 0])
    if k % 512:
        return np.exp2(np.random.permutation(np.resize(levels, k // 32))).repeat(32)
    a = np.empty((k // 512, 16))
    for p in range(k // 512):
        a[p, :8] = np.random.permutation(np.resize(levels, 8))
        for g in range(8):
            far = levels[np.abs(levels - a[p, g]) >= 10]
            a[p, g + 8] = far[np.random.randint(len(far))]
    return np.exp2(a.ravel()).repeat(32)


def f64(x):
    return np.asarray(x).astype(np.float64)


def striped(idx):
    return np.tile(idx.reshape(-1, 16).T, (8, 1)).astype(np.uint16)


def unstriped(offs):
    return offs[:16].T.reshape(-1).astype(np.int64)


E2M1 = np.array([0.0, 0.5, 1.0, 1.5, 2.0, 3.0, 4.0, 6.0, -0.0, -0.5, -1.0, -1.5, -2.0, -3.0, -4.0, -6.0])


def pack_weight(w, fmt):
    k, n = w.shape
    w = f64(np.asarray(w, np.float32).astype(ml_dtypes.bfloat16)).reshape(k // 32, 32, n)
    amax = np.abs(w).max(1)
    if fmt == "e4m3":
        byte = np.frexp(amax)[1] - 1 + 127 - 7
    else:
        mant, ex = np.frexp(amax / 6.0)
        byte = np.where(mant > 0.5, ex, ex - 1) + 127
    byte = np.clip(np.where(amax > 0, byte, 1), 1, 254)
    scaled = (w * np.exp2(127.0 - byte)[:, None, :]).reshape(k, n).astype(np.float32)
    by_word = np.ascontiguousarray(scaled.reshape(k // 512, 128, 4, n).transpose(0, 1, 3, 2))
    if fmt == "e4m3":
        words = by_word.astype(ml_dtypes.float8_e4m3fn).view(np.uint8)
    else:
        c = by_word.astype(ml_dtypes.float4_e2m1fn).view(np.uint8) & 0xF
        words = (c[..., 0::2] | (c[..., 1::2] << 4)).reshape(k // 512, 128, 2 * n)
    return np.ascontiguousarray(words), np.ascontiguousarray(byte.astype(np.uint8).reshape(k // 512, 16, n))


def unpack_weight(words, scales, fmt):
    g, _, n = scales.shape
    words = np.ascontiguousarray(words).reshape(g, 128, n, -1)
    if fmt == "e4m3":
        vals = words.view(ml_dtypes.float8_e4m3fn).astype(np.float64)
    else:
        nib = np.empty((g, 128, n, 4), np.uint8)
        nib[..., 0::2] = words & 0xF
        nib[..., 1::2] = words >> 4
        vals = E2M1[nib]
    vals = vals * np.repeat(np.exp2(scales.astype(np.float64) - 127.0), 8, axis=1)[..., None]
    return vals.transpose(0, 1, 3, 2).reshape(g * 512, n)


def gelu(v):
    return 0.5 * v * (1.0 + np.tanh(np.sqrt(2.0 / np.pi) * (v + 0.044715 * v**3)))


K, T, S, H, N = 1536, 4096, 512, 1024, 384

def setup_inputs():
    n = np.random.standard_normal
    s = mx_kscale(K)[:, None]
    u = mx_kscale(H)[:, None]
    tab_words, tab_scales = pack_weight(n((K, T)) * s, "e4m3")
    w1_words, w1_scales = pack_weight(n((K, H)) / np.sqrt(K) / s * u.T, "e2m1")
    w2 = (n((H, N)) / np.sqrt(H) / u).astype(np.float32)
    offs = striped(np.random.permutation(T)[:S])
    offs2 = striped(np.random.permutation(T)[:S])
    offs3 = striped(np.random.permutation(T)[:S])
    return {"tab_words": tab_words, "tab_scales": tab_scales,
            "w1_words": w1_words, "w1_scales": w1_scales, "w2": w2,
            "offs": offs, "offs2": offs2, "offs3": offs3}

def reference(tab_words, tab_scales, w1_words, w1_scales, w2, offs, offs2, offs3):
    TW = unpack_weight(tab_words, tab_scales, "e4m3")
    v = TW[:, unstriped(offs)]
    v2 = TW[:, unstriped(offs2)]
    v3 = TW[:, unstriped(offs3)]
    w1 = unpack_weight(w1_words, w1_scales, "e2m1")
    f1 = w1.T @ v
    f2 = w1.T @ v2
    f3 = w1.T @ v3
    high = np.maximum(np.maximum(f1, f2), f3)
    low = np.minimum(np.minimum(f1, f2), f3)
    h = mxq(high - low, 0, "e4m3")
    w2q = mxq(f64(w2), 0, "e4m3")
    return w2q.T @ h

@@ -1,0 +1,227 @@
+from contextlib import ExitStack
+
+import concourse.mybir as mybir
+from concourse.masks import make_identity
+
+K, T, S, H, N = 1536, 4096, 512, 1024, 384
+FLOPS = 2 * (3 * K * H * S + H * N * S)
+
+F32 = mybir.dt.float32
+BF16 = mybir.dt.bfloat16
+I32 = mybir.dt.int32
+U32 = mybir.dt.uint32
+U16 = mybir.dt.uint16
+U8 = mybir.dt.uint8
+FP8X4 = mybir.dt.float8_e4m3fn_x4
+FP4X4 = mybir.dt.float4_e2m1fn_x4
+MAX = mybir.AluOpType.max
+MIN = mybir.AluOpType.min
+SUB = mybir.AluOpType.subtract
+
+P = 128
+PASS = 512
+KP = K // PASS
+HP = H // PASS
+LISTS = 3
+JB = S // P
+NB = N // P
+UNITS = HP * JB
+ROW0 = P - 16 * KP
+
+
+def tile_list_peer_clock_disagreement_kernel(
+    tc, tab_words, tab_scales, w1_words, w1_scales, w2, offs, offs2, offs3, out
+):
+    nc = tc.nc
+    with ExitStack() as ctx:
+        keep = ctx.enter_context(tc.tile_pool(name="keep", bufs=1))
+        ring = ctx.enter_context(tc.tile_pool(name="ring", bufs=3))
+        psum = ctx.enter_context(tc.psum_pool(name="psum", bufs=1))
+
+        lists = [keep.tile([P, S // 16], U16, name="list%d" % l) for l in range(LISTS)]
+        tab = [keep.tile([P, T], U32, name="tab%d" % a, align_bytes=64) for a in range(KP)]
+        tab_sc = keep.tile([P, T], U8, name="tab_sc", align_bytes=64)
+        picked_sc = keep.tile([P, LISTS * S], U8, name="picked_sc", align_bytes=64)
+        v_sc = keep.tile([P, KP, LISTS * S], U8, name="v_sc", align_bytes=64)
+        v = [[keep.tile([P, S], U32, name="v%d_%d" % (l, a), align_bytes=64) for a in range(KP)] for l in range(LISTS)]
+        w1 = [keep.tile([P, KP, 2 * PASS], U8, name="w1_%d" % b, align_bytes=64) for b in range(HP)]
+        w1_sc = keep.tile([P, KP, H], U8, name="w1_sc", align_bytes=64)
+        w2_raw = keep.tile([P, HP, 4, N], F32, name="w2_raw", align_bytes=64)
+        w2_bf = [keep.tile([P, N, 4], BF16, name="w2_bf%d" % b, align_bytes=64) for b in range(HP)]
+        w2_q = [keep.tile([P, N], U32, name="w2_q%d" % b, align_bytes=64) for b in range(HP)]
+        w2_sc = [keep.tile([P, N], U8, name="w2_sc%d" % b, align_bytes=64) for b in range(HP)]
+        h_q = [keep.tile([P, P], U32, name="h_q%d" % u, align_bytes=64) for u in range(UNITS)]
+        h_sc = [keep.tile([P, P], U8, name="h_sc%d" % u, align_bytes=64) for u in range(UNITS)]
+        ident = keep.tile([P, P], F32, name="ident", align_bytes=64)
+
+        def load_tab(a):
+            nc.sync.dma_start(out=tab[a][:].bitcast(I32), in_=tab_words[a].rearrange("p t i -> p (t i)").bitcast(I32))
+
+        def load_w1(b):
+            cols = w1_words[:, :, 2 * PASS * b : 2 * PASS * (b + 1)]
+            nc.sync.dma_start(out=w1[b][:].bitcast(I32), in_=cols.rearrange("a p n -> p a n").bitcast(I32))
+
+        for a in range(KP):
+            nc.sync.dma_start(out=tab_sc[ROW0 + a : P : KP, :].bitcast(I32), in_=tab_scales[a].bitcast(I32))
+        nc.sync.dma_start(lists[0][:], offs)
+        load_tab(0)
+        nc.sync.dma_start(lists[1][:], offs2)
+        nc.sync.dma_start(lists[2][:], offs3)
+        load_w1(0)
+        load_tab(1)
+        load_tab(2)
+        load_w1(1)
+        nc.sync.dma_start(out=w2_raw[:], in_=w2.rearrange("(b p t) n -> p b t n", b=HP, t=4))
+
+        nc.vector.memset(tab_sc[0:64, :].bitcast(I32), 0)
+        nc.vector.memset(tab_sc[64:ROW0, :].bitcast(I32), 0)
+        nc.vector.memset(v_sc[:].bitcast(I32), 0)
+        nc.gpsimd.memset(w1_sc[:].bitcast(I32), 0)
+        for q in range(4):
+            rows = w1_scales[:, 4 * q : 4 * q + 4, :].rearrange("a r n -> r a n")
+            nc.gpsimd.dma_start(out=w1_sc[32 * q : 32 * q + 4].bitcast(I32), in_=rows.bitcast(I32))
+        make_identity(nc, ident[:])
+
+        for l in range(LISTS):
+            nc.vector.tensor_copy(picked_sc[:, S * l : S * (l + 1)], tab_sc[:].indirect(lists[l][:]))
+        for q in range(4):
+            first = ROW0 + 4 * KP * q
+            nc.scalar.dma_start(
+                out=v_sc[32 * q : 32 * q + 4].bitcast(I32),
+                in_=picked_sc[first : first + 4 * KP, :].bitcast(I32),
+            )
+        for a in range(KP):
+            for l in range(LISTS):
+                nc.vector.tensor_copy(v[l][a][:], tab[a][:].indirect(lists[l][:]))
+
+        f = {}
+        first_copy = {}
+        high = {}
+        low = {}
+        h_t = {}
+        h_bf = {}
+
+        def product(u, l, passes):
+            b, jb = divmod(u, JB)
+            if (u, l) not in f:
+                f[(u, l)] = psum.tile([P, PASS], F32, name="f%d" % l, tag="f%d" % l, bufs=2)
+            for a in passes:
+                c0 = S * l + P * jb
+                nc.tensor.matmul_mx(
+                    out=f[(u, l)][:],
+                    lhsT=v[l][a][:, P * jb : P * (jb + 1)].bitcast(FP8X4),
+                    lhsT_scale=v_sc[:, a, c0 : c0 + P],
+                    rhs=w1[b][:, a, :].bitcast(FP4X4),
+                    rhs_scale=w1_sc[:, a, PASS * b : PASS * (b + 1)],
+                    start=(a == 0),
+                    stop=(a == KP - 1),
+                )
+
+        def dealt(u, l):
+            return f[(u, l)][:].rearrange("j (q u e) -> j u q e", u=2, e=2)
+
+        def flat(t):
+            return t[:].rearrange("j (u q e) -> j u q e", u=2, e=2)
+
+        def copy_first(u):
+            first_copy[u] = ring.tile([P, PASS], F32, name="first_copy", tag="first_copy", bufs=4)
+            nc.scalar.copy(out=flat(first_copy[u]), in_=dealt(u, 0))
+
+        def extremes_of_two(u):
+            high[u] = ring.tile([P, PASS], F32, name="high2", tag="high2", bufs=2)
+            low[u] = ring.tile([P, PASS], F32, name="low2", tag="low2", bufs=2)
+            nc.vector.tensor_tensor(flat(high[u]), dealt(u, 1), flat(first_copy[u]), MAX)
+            nc.vector.tensor_tensor(flat(low[u]), dealt(u, 1), flat(first_copy[u]), MIN)
+
+        def spread(u):
+            high3 = ring.tile([P, PASS], F32, name="high3", tag="high3", bufs=2)
+            low3 = ring.tile([P, PASS], F32, name="low3", tag="low3", bufs=2)
+            nc.vector.tensor_tensor(flat(high3), dealt(u, 2), flat(high[u]), MAX)
+            nc.vector.tensor_tensor(flat(low3), dealt(u, 2), flat(low[u]), MIN)
+            h_t[u] = ring.tile([P, PASS], BF16, name="h_t", tag="h_t", bufs=2, align_bytes=64)
+            engine = nc.vector if u == UNITS - 1 else nc.gpsimd
+            engine.tensor_tensor(h_t[u][:], high3[:], low3[:], SUB)
+
+        def turn(u):
+            words = h_t[u][:].bitcast(F32)
+            turned = psum.tile([P, 2, P], F32, name="turned", tag="turned")
+            for half in range(2):
+                nc.tensor.transpose(turned[:, half, :], words[:, P * half : P * (half + 1)], ident[:])
+            h_bf[u] = ring.tile([P, 4 * P], BF16, name="h_bf", tag="h_bf", bufs=2, align_bytes=64)
+            nc.scalar.copy(
+                out=h_bf[u][:].bitcast(F32).rearrange("q (j u) -> q j u", u=2),
+                in_=turned[:].rearrange("q u j -> q j u"),
+            )
+
+        def quantise_h(u):
+            nc.vector.quantize_mx(out=h_q[u][:].bitcast(FP8X4), scales=h_sc[u][:], in_=h_bf[u][:])
+
+        def round_w2(piece):
+            b, m = divmod(piece, NB)
+            cols = slice(P * m, P * (m + 1))
+            nc.scalar.copy(
+                out=w2_bf[b][:, cols, :].rearrange("p (c i) t -> p c t i", i=4),
+                in_=w2_raw[:, b, :, cols].rearrange("p t (c i) -> p c t i", i=4),
+            )
+
+        def quantise_w2(b):
+            nc.vector.quantize_mx(
+                out=w2_q[b][:].bitcast(FP8X4), scales=w2_sc[b][:], in_=w2_bf[b][:].rearrange("p n t -> p (n t)")
+            )
+
+        def scores(jb):
+            acc = psum.tile([P, NB, P], F32, name="acc", tag="acc")
+            for m in range(NB):
+                cols = slice(P * m, P * (m + 1))
+                for b in range(HP):
+                    nc.tensor.matmul_mx(
+                        out=acc[:, m, :],
+                        lhsT=w2_q[b][:, cols].bitcast(FP8X4),
+                        lhsT_scale=w2_sc[b][:, cols],
+                        rhs=h_q[JB * b + jb][:].bitcast(FP8X4),
+                        rhs_scale=h_sc[JB * b + jb][:],
+                        start=(b == 0),
+                        stop=(b == HP - 1),
+                    )
+            result = ring.tile([P, NB, P], F32, name="result", tag="result", bufs=2)
+            nc.scalar.copy(out=result[:], in_=acc[:])
+            nc.sync.dma_start(
+                out=out.rearrange("(m p) j -> p m j", p=P)[:, :, P * jb : P * (jb + 1)], in_=result[:]
+            )
+
+        for a in range(KP - 1):
+            for l in range(LISTS):
+                for u in range(2):
+                    product(u, l, [a])
+        for u in range(2):
+            product(u, 0, [KP - 1])
+            copy_first(u)
+        product(2, 0, range(KP))
+        copy_first(2)
+        for l in range(1, LISTS):
+            for u in range(2):
+                product(u, l, [KP - 1])
+
+        for u in range(UNITS + 2):
+            if u < UNITS:
+                extremes_of_two(u)
+            if u >= 2:
+                quantise_h(u - 2)
+            if 3 <= u < 3 + HP:
+                quantise_w2(u - 3)
+            if 1 <= u <= UNITS:
+                turn(u - 1)
+            if u - 2 >= JB:
+                scores(u - 2 - JB)
+            if u + 2 < UNITS:
+                product(u + 2, 1, range(KP))
+            if u < UNITS:
+                spread(u)
+            if u + 2 < UNITS:
+                product(u + 2, 2, range(KP))
+            if u + 3 < UNITS:
+                product(u + 3, 0, range(KP))
+                copy_first(u + 3)
+            if 1 <= u <= 3:
+                round_w2(2 * u - 2)
+                round_w2(2 * u - 1)

@@ -36,17 +36,21 @@ def tile_list_peer_clock_disagreement_kernel(
     with ExitStack() as ctx:
         keep = ctx.enter_context(tc.tile_pool(name="keep", bufs=1))
         ring = ctx.enter_context(tc.tile_pool(name="ring", bufs=3))
+        reuse = ctx.enter_context(tc.tile_pool(name="reuse", bufs=1))
         psum = ctx.enter_context(tc.psum_pool(name="psum", bufs=1))
 
         lists = [keep.tile([P, S // 16], U16, name="list%d" % l) for l in range(LISTS)]
-        tab = [keep.tile([P, T], U32, name="tab%d" % a, align_bytes=64) for a in range(KP)]
-        tab_sc = keep.tile([P, T], U8, name="tab_sc", align_bytes=64)
+        tab = [reuse.tile([P, T], U32, name="tab%d" % a, align_bytes=64, offset=4 * T * a) for a in range(KP)]
+        tab_sc = reuse.tile([P, T], U8, name="tab_sc", align_bytes=64, offset=4 * T * (KP - 1))
         picked_sc = keep.tile([P, LISTS * S], U8, name="picked_sc", align_bytes=64)
         v_sc = keep.tile([P, KP, LISTS * S], U8, name="v_sc", align_bytes=64)
         v = [[keep.tile([P, S], U32, name="v%d_%d" % (l, a), align_bytes=64) for a in range(KP)] for l in range(LISTS)]
-        w1 = [keep.tile([P, KP, 2 * PASS], U8, name="w1_%d" % b, align_bytes=64) for b in range(HP)]
+        w1 = [
+            keep.tile([P, KP, 2 * PASS], U8, name="w1_0", align_bytes=64),
+            reuse.tile([P, KP, 2 * PASS], U8, name="w1_1", align_bytes=64, offset=0),
+        ]
         w1_sc = keep.tile([P, KP, H], U8, name="w1_sc", align_bytes=64)
-        w2_raw = keep.tile([P, HP, 4, N], F32, name="w2_raw", align_bytes=64)
+        w2_raw = reuse.tile([P, HP, 4, N], F32, name="w2_raw", align_bytes=64, offset=T)
         w2_bf = [keep.tile([P, N, 4], BF16, name="w2_bf%d" % b, align_bytes=64) for b in range(HP)]
         w2_q = [keep.tile([P, N], U32, name="w2_q%d" % b, align_bytes=64) for b in range(HP)]
         w2_sc = [keep.tile([P, N], U8, name="w2_sc%d" % b, align_bytes=64) for b in range(HP)]
@@ -62,17 +66,12 @@ def tile_list_peer_clock_disagreement_kernel(
             nc.sync.dma_start(out=w1[b][:].bitcast(I32), in_=cols.rearrange("a p n -> p a n").bitcast(I32))
 
         for a in range(KP):
-            nc.sync.dma_start(out=tab_sc[ROW0 + a : P : KP, :].bitcast(I32), in_=tab_scales[a].bitcast(I32))
-        nc.sync.dma_start(lists[0][:], offs)
+            nc.scalar.dma_start(out=tab_sc[ROW0 + a : P : KP, :].bitcast(I32), in_=tab_scales[a].bitcast(I32))
+        for tile, src in zip(lists, (offs, offs2, offs3)):
+            nc.sync.dma_start(tile[:], src)
         load_tab(0)
-        nc.sync.dma_start(lists[1][:], offs2)
-        nc.sync.dma_start(lists[2][:], offs3)
         load_w1(0)
         load_tab(1)
-        load_tab(2)
-        load_w1(1)
-        nc.sync.dma_start(out=w2_raw[:], in_=w2.rearrange("(b p t) n -> p b t n", b=HP, t=4))
-
         nc.vector.memset(tab_sc[0:64, :].bitcast(I32), 0)
         nc.vector.memset(tab_sc[64:ROW0, :].bitcast(I32), 0)
         nc.vector.memset(v_sc[:].bitcast(I32), 0)
@@ -86,13 +85,18 @@ def tile_list_peer_clock_disagreement_kernel(
             nc.vector.tensor_copy(picked_sc[:, S * l : S * (l + 1)], tab_sc[:].indirect(lists[l][:]))
         for q in range(4):
             first = ROW0 + 4 * KP * q
-            nc.scalar.dma_start(
+            queue = nc.sync if q % 2 == 0 else nc.scalar
+            queue.dma_start(
                 out=v_sc[32 * q : 32 * q + 4].bitcast(I32),
                 in_=picked_sc[first : first + 4 * KP, :].bitcast(I32),
             )
+        load_tab(2)
         for a in range(KP):
             for l in range(LISTS):
                 nc.vector.tensor_copy(v[l][a][:], tab[a][:].indirect(lists[l][:]))
+            if a == 0:
+                load_w1(1)
+                nc.sync.dma_start(out=w2_raw[:], in_=w2.rearrange("(b p t) n -> p b t n", b=HP, t=4))
 
         f = {}
         first_copy = {}
@@ -104,7 +108,10 @@ def tile_list_peer_clock_disagreement_kernel(
         def product(u, l, passes):
             b, jb = divmod(u, JB)
             if (u, l) not in f:
-                f[(u, l)] = psum.tile([P, PASS], F32, name="f%d" % l, tag="f%d" % l, bufs=2)
+                if l == 0 and u in (2, 3):
+                    f[(u, l)] = psum.tile([P, PASS], F32, name="f_early", tag=("turned", "acc")[u - 2])
+                else:
+                    f[(u, l)] = psum.tile([P, PASS], F32, name="f%d" % l, tag="f%d" % l, bufs=2)
             for a in passes:
                 c0 = S * l + P * jb
                 nc.tensor.matmul_mx(
@@ -124,7 +131,7 @@ def tile_list_peer_clock_disagreement_kernel(
             return t[:].rearrange("j (u q e) -> j u q e", u=2, e=2)
 
         def copy_first(u):
-            first_copy[u] = ring.tile([P, PASS], F32, name="first_copy", tag="first_copy", bufs=4)
+            first_copy[u] = ring.tile([P, PASS], F32, name="first_copy", tag="first_copy", bufs=UNITS)
             nc.scalar.copy(out=flat(first_copy[u]), in_=dealt(u, 0))
 
         def extremes_of_two(u):
@@ -169,38 +176,42 @@ def tile_list_peer_clock_disagreement_kernel(
                 out=w2_q[b][:].bitcast(FP8X4), scales=w2_sc[b][:], in_=w2_bf[b][:].rearrange("p n t -> p (n t)")
             )
 
-        def scores(jb):
-            acc = psum.tile([P, NB, P], F32, name="acc", tag="acc")
+        acc = {}
+
+        def score_passes(jb, b):
+            if b == 0:
+                acc[jb] = psum.tile([P, NB, P], F32, name="acc", tag="acc")
             for m in range(NB):
                 cols = slice(P * m, P * (m + 1))
-                for b in range(HP):
-                    nc.tensor.matmul_mx(
-                        out=acc[:, m, :],
-                        lhsT=w2_q[b][:, cols].bitcast(FP8X4),
-                        lhsT_scale=w2_sc[b][:, cols],
-                        rhs=h_q[JB * b + jb][:].bitcast(FP8X4),
-                        rhs_scale=h_sc[JB * b + jb][:],
-                        start=(b == 0),
-                        stop=(b == HP - 1),
-                    )
+                nc.tensor.matmul_mx(
+                    out=acc[jb][:, m, :],
+                    lhsT=w2_q[b][:, cols].bitcast(FP8X4),
+                    lhsT_scale=w2_sc[b][:, cols],
+                    rhs=h_q[JB * b + jb][:].bitcast(FP8X4),
+                    rhs_scale=h_sc[JB * b + jb][:],
+                    start=(b == 0 and m == 0),
+                    stop=(b == HP - 1 and m == NB - 1),
+                )
+
+        def store(jb):
             result = ring.tile([P, NB, P], F32, name="result", tag="result", bufs=2)
-            nc.scalar.copy(out=result[:], in_=acc[:])
+            nc.scalar.copy(out=result[:], in_=acc[jb][:])
             nc.sync.dma_start(
                 out=out.rearrange("(m p) j -> p m j", p=P)[:, :, P * jb : P * (jb + 1)], in_=result[:]
             )
 
         for a in range(KP - 1):
             for l in range(LISTS):
-                for u in range(2):
+                for u in range(JB if l == 0 else 2):
                     product(u, l, [a])
-        for u in range(2):
+        for u in range(JB):
             product(u, 0, [KP - 1])
             copy_first(u)
-        product(2, 0, range(KP))
-        copy_first(2)
         for l in range(1, LISTS):
             for u in range(2):
                 product(u, l, [KP - 1])
+            product(JB + l - 1, 0, range(KP))
+            copy_first(JB + l - 1)
 
         for u in range(UNITS + 2):
             if u < UNITS:
@@ -209,19 +220,22 @@ def tile_list_peer_clock_disagreement_kernel(
                 quantise_h(u - 2)
             if 3 <= u < 3 + HP:
                 quantise_w2(u - 3)
+            if u - 2 >= JB:
+                score_passes(u - 2 - JB, 1)
+                store(u - 2 - JB)
             if 1 <= u <= UNITS:
                 turn(u - 1)
-            if u - 2 >= JB:
-                scores(u - 2 - JB)
+            if JB <= u - 1 < UNITS:
+                score_passes(u - 1 - JB, 0)
             if u + 2 < UNITS:
                 product(u + 2, 1, range(KP))
             if u < UNITS:
                 spread(u)
             if u + 2 < UNITS:
                 product(u + 2, 2, range(KP))
-            if u + 3 < UNITS:
-                product(u + 3, 0, range(KP))
-                copy_first(u + 3)
+            if u + 6 < UNITS:
+                product(u + 6, 0, range(KP))
+                copy_first(u + 6)
             if 1 <= u <= 3:
                 round_w2(2 * u - 2)
                 round_w2(2 * u - 1)

@@ -27,6 +27,8 @@ JB = S // P
 NB = N // P
 UNITS = HP * JB
 ROW0 = P - 16 * KP
+ORDER = [(0, 0), (1, 0), (0, 1), (1, 1), (2, 0), (2, 1), (3, 0), (3, 1)]
+EARLY = (4, 6)
 
 
 def tile_list_peer_clock_disagreement_kernel(
@@ -54,8 +56,6 @@ def tile_list_peer_clock_disagreement_kernel(
         w2_bf = [keep.tile([P, N, 4], BF16, name="w2_bf%d" % b, align_bytes=64) for b in range(HP)]
         w2_q = [keep.tile([P, N], U32, name="w2_q%d" % b, align_bytes=64) for b in range(HP)]
         w2_sc = [keep.tile([P, N], U8, name="w2_sc%d" % b, align_bytes=64) for b in range(HP)]
-        h_q = [keep.tile([P, P], U32, name="h_q%d" % u, align_bytes=64) for u in range(UNITS)]
-        h_sc = [keep.tile([P, P], U8, name="h_sc%d" % u, align_bytes=64) for u in range(UNITS)]
         ident = keep.tile([P, P], F32, name="ident", align_bytes=64)
 
         def load_tab(a):
@@ -102,14 +102,17 @@ def tile_list_peer_clock_disagreement_kernel(
         first_copy = {}
         high = {}
         low = {}
+        high3 = {}
+        h_q = {}
+        h_sc = {}
         h_t = {}
         h_bf = {}
 
         def product(u, l, passes):
-            b, jb = divmod(u, JB)
+            jb, b = ORDER[u]
             if (u, l) not in f:
-                if l == 0 and u in (2, 3):
-                    f[(u, l)] = psum.tile([P, PASS], F32, name="f_early", tag=("turned", "acc")[u - 2])
+                if l == 0 and u in EARLY:
+                    f[(u, l)] = psum.tile([P, PASS], F32, name="f_early", tag=("turned", "acc")[EARLY.index(u)])
                 else:
                     f[(u, l)] = psum.tile([P, PASS], F32, name="f%d" % l, tag="f%d" % l, bufs=2)
             for a in passes:
@@ -140,35 +143,45 @@ def tile_list_peer_clock_disagreement_kernel(
             nc.vector.tensor_tensor(flat(high[u]), dealt(u, 1), flat(first_copy[u]), MAX)
             nc.vector.tensor_tensor(flat(low[u]), dealt(u, 1), flat(first_copy[u]), MIN)
 
-        def spread(u):
-            high3 = ring.tile([P, PASS], F32, name="high3", tag="high3", bufs=2)
-            low3 = ring.tile([P, PASS], F32, name="low3", tag="low3", bufs=2)
-            nc.vector.tensor_tensor(flat(high3), dealt(u, 2), flat(high[u]), MAX)
-            nc.vector.tensor_tensor(flat(low3), dealt(u, 2), flat(low[u]), MIN)
-            h_t[u] = ring.tile([P, PASS], BF16, name="h_t", tag="h_t", bufs=2, align_bytes=64)
-            engine = nc.vector if u == UNITS - 1 else nc.gpsimd
-            engine.tensor_tensor(h_t[u][:], high3[:], low3[:], SUB)
+        def third_high(u):
+            high3[u] = ring.tile([P, PASS], F32, name="high3", tag="high3", bufs=2)
+            nc.vector.tensor_tensor(flat(high3[u]), dealt(u, 2), flat(high[u]), MAX)
 
-        def turn(u):
-            words = h_t[u][:].bitcast(F32)
-            turned = psum.tile([P, 2, P], F32, name="turned", tag="turned")
-            for half in range(2):
-                nc.tensor.transpose(turned[:, half, :], words[:, P * half : P * (half + 1)], ident[:])
-            h_bf[u] = ring.tile([P, 4 * P], BF16, name="h_bf", tag="h_bf", bufs=2, align_bytes=64)
+        def spread(u):
+            low3 = ring.tile([P, PASS], F32, name="low3", tag="low3", bufs=2)
+            nc.vector.tensor_tensor(flat(low3), dealt(u, 2), flat(low[u]), MIN)
+            h_t[u] = ring.tile([P, PASS], BF16, name="h_t", tag="h_t", bufs=3, align_bytes=64)
+            engine = nc.vector if u == UNITS - 1 else nc.gpsimd
+            engine.tensor_tensor(h_t[u][:], high3[u][:], low3[:], SUB)
+
+        def turn(units):
+            n = len(units)
+            turned = psum.tile([P, n, 2, P], F32, name="turned", tag="turned")
+            for k, u in enumerate(units):
+                words = h_t[u][:].bitcast(F32)
+                for half in range(2):
+                    nc.tensor.transpose(turned[:, k, half, :], words[:, P * half : P * (half + 1)], ident[:])
+            h_bf[units] = ring.tile([P, n * 4 * P], BF16, name="h_bf", tag="h_bf", bufs=3, align_bytes=64)
             nc.scalar.copy(
-                out=h_bf[u][:].bitcast(F32).rearrange("q (j u) -> q j u", u=2),
-                in_=turned[:].rearrange("q u j -> q j u"),
+                out=h_bf[units][:].bitcast(F32).rearrange("q (k j u) -> q k j u", k=n, u=2),
+                in_=turned[:].rearrange("q k u j -> q k j u"),
             )
 
-        def quantise_h(u):
-            nc.vector.quantize_mx(out=h_q[u][:].bitcast(FP8X4), scales=h_sc[u][:], in_=h_bf[u][:])
+        def quantise_h(units):
+            n = len(units)
+            codes = keep.tile([P, n * P], U32, name="h_q%d" % units[0], align_bytes=64)
+            scales = keep.tile([P, n * P], U8, name="h_sc%d" % units[0], align_bytes=64)
+            nc.vector.quantize_mx(out=codes[:].bitcast(FP8X4), scales=scales[:], in_=h_bf[units][:])
+            for k, u in enumerate(units):
+                h_q[ORDER[u]] = codes[:, P * k : P * (k + 1)]
+                h_sc[ORDER[u]] = scales[:, P * k : P * (k + 1)]
 
         def round_w2(piece):
             b, m = divmod(piece, NB)
             cols = slice(P * m, P * (m + 1))
             nc.scalar.copy(
-                out=w2_bf[b][:, cols, :].rearrange("p (c i) t -> p c t i", i=4),
-                in_=w2_raw[:, b, :, cols].rearrange("p t (c i) -> p c t i", i=4),
+                out=w2_bf[b][:, cols, :],
+                in_=w2_raw[:, b, :, cols].rearrange("p t n -> p n t"),
             )
 
         def quantise_w2(b):
@@ -180,15 +193,15 @@ def tile_list_peer_clock_disagreement_kernel(
 
         def score_passes(jb, b):
             if b == 0:
-                acc[jb] = psum.tile([P, NB, P], F32, name="acc", tag="acc")
+                acc[jb] = psum.tile([P, NB, P], F32, name="acc", tag="f0", bufs=2)
             for m in range(NB):
                 cols = slice(P * m, P * (m + 1))
                 nc.tensor.matmul_mx(
                     out=acc[jb][:, m, :],
                     lhsT=w2_q[b][:, cols].bitcast(FP8X4),
                     lhsT_scale=w2_sc[b][:, cols],
-                    rhs=h_q[JB * b + jb][:].bitcast(FP8X4),
-                    rhs_scale=h_sc[JB * b + jb][:],
+                    rhs=h_q[(jb, b)].bitcast(FP8X4),
+                    rhs_scale=h_sc[(jb, b)],
                     start=(b == 0 and m == 0),
                     stop=(b == HP - 1 and m == NB - 1),
                 )
@@ -200,42 +213,54 @@ def tile_list_peer_clock_disagreement_kernel(
                 out=out.rearrange("(m p) j -> p m j", p=P)[:, :, P * jb : P * (jb + 1)], in_=result[:]
             )
 
+        def scores(jb):
+            for b in range(HP):
+                score_passes(jb, b)
+            store(jb)
+
         for a in range(KP - 1):
             for l in range(LISTS):
-                for u in range(JB if l == 0 else 2):
+                for u in (0, 1) + (EARLY if l == 0 else ()):
                     product(u, l, [a])
-        for u in range(JB):
+        for u in (0, 1) + EARLY:
             product(u, 0, [KP - 1])
             copy_first(u)
         for l in range(1, LISTS):
             for u in range(2):
                 product(u, l, [KP - 1])
-            product(JB + l - 1, 0, range(KP))
-            copy_first(JB + l - 1)
+            product(l + 1, 0, range(KP))
+            copy_first(l + 1)
 
-        for u in range(UNITS + 2):
-            if u < UNITS:
-                extremes_of_two(u)
-            if u >= 2:
-                quantise_h(u - 2)
-            if 3 <= u < 3 + HP:
-                quantise_w2(u - 3)
-            if u - 2 >= JB:
-                score_passes(u - 2 - JB, 1)
-                store(u - 2 - JB)
-            if 1 <= u <= UNITS:
-                turn(u - 1)
-            if JB <= u - 1 < UNITS:
-                score_passes(u - 1 - JB, 0)
+        for u in range(UNITS):
+            extremes_of_two(u)
+            if u in (2, 4, 6):
+                turn((u - 2, u - 1))
+            if u == UNITS - 1:
+                turn((u - 1,))
             if u + 2 < UNITS:
                 product(u + 2, 1, range(KP))
-            if u < UNITS:
-                spread(u)
+            third_high(u)
+            if u in (2, 4):
+                quantise_w2(u // 2 - 1)
+            if u in (3, 5):
+                quantise_h((u - 3, u - 2))
+            spread(u)
             if u + 2 < UNITS:
                 product(u + 2, 2, range(KP))
-            if u + 6 < UNITS:
-                product(u + 6, 0, range(KP))
-                copy_first(u + 6)
-            if 1 <= u <= 3:
-                round_w2(2 * u - 2)
-                round_w2(2 * u - 1)
+            if u < 2:
+                product(5 + 2 * u, 0, range(KP))
+                copy_first(5 + 2 * u)
+            if u in (0, 2):
+                for m in range(NB):
+                    round_w2(NB * (u // 2) + m)
+            if u == 5:
+                scores(0)
+                scores(1)
+        turn((7,))
+        quantise_h((4, 5))
+        quantise_h((6,))
+        scores(2)
+        score_passes(3, 0)
+        quantise_h((7,))
+        score_passes(3, 1)
+        store(3)

@@ -47,10 +47,10 @@ def tile_list_peer_clock_disagreement_kernel(
         picked_sc = keep.tile([P, LISTS * S], U8, name="picked_sc", align_bytes=64)
         v_sc = keep.tile([P, KP, LISTS * S], U8, name="v_sc", align_bytes=64)
         v = [[keep.tile([P, S], U32, name="v%d_%d" % (l, a), align_bytes=64) for a in range(KP)] for l in range(LISTS)]
-        w1 = [
-            keep.tile([P, KP, 2 * PASS], U8, name="w1_0", align_bytes=64),
-            reuse.tile([P, KP, 2 * PASS], U8, name="w1_1", align_bytes=64, offset=0),
-        ]
+        w1_early = keep.tile([P, KP - 1, 2 * PASS], U8, name="w1_early", align_bytes=64)
+        w1_last = reuse.tile([P, 1, 2 * PASS], U8, name="w1_last", align_bytes=64, offset=0)
+        w1_upper = reuse.tile([P, KP, 2 * PASS], U8, name="w1_upper", align_bytes=64, offset=2 * PASS)
+        w1 = [[w1_early[:, 0, :], w1_early[:, 1, :], w1_last[:, 0, :]], [w1_upper[:, a, :] for a in range(KP)]]
         w1_sc = keep.tile([P, KP, H], U8, name="w1_sc", align_bytes=64)
         w2_raw = reuse.tile([P, HP, 4, N], F32, name="w2_raw", align_bytes=64, offset=T)
         w2_bf = [keep.tile([P, N, 4], BF16, name="w2_bf%d" % b, align_bytes=64) for b in range(HP)]
@@ -61,16 +61,16 @@ def tile_list_peer_clock_disagreement_kernel(
         def load_tab(a):
             nc.sync.dma_start(out=tab[a][:].bitcast(I32), in_=tab_words[a].rearrange("p t i -> p (t i)").bitcast(I32))
 
-        def load_w1(b):
-            cols = w1_words[:, :, 2 * PASS * b : 2 * PASS * (b + 1)]
-            nc.sync.dma_start(out=w1[b][:].bitcast(I32), in_=cols.rearrange("a p n -> p a n").bitcast(I32))
+        def load_w1(tile, passes, b):
+            cols = w1_words[passes, :, 2 * PASS * b : 2 * PASS * (b + 1)]
+            nc.sync.dma_start(out=tile[:].bitcast(I32), in_=cols.rearrange("a p n -> p a n").bitcast(I32))
 
         for a in range(KP):
             nc.scalar.dma_start(out=tab_sc[ROW0 + a : P : KP, :].bitcast(I32), in_=tab_scales[a].bitcast(I32))
         for tile, src in zip(lists, (offs, offs2, offs3)):
             nc.sync.dma_start(tile[:], src)
         load_tab(0)
-        load_w1(0)
+        load_w1(w1_early, slice(0, KP - 1), 0)
         load_tab(1)
         nc.vector.memset(tab_sc[0:64, :].bitcast(I32), 0)
         nc.vector.memset(tab_sc[64:ROW0, :].bitcast(I32), 0)
@@ -95,7 +95,8 @@ def tile_list_peer_clock_disagreement_kernel(
             for l in range(LISTS):
                 nc.vector.tensor_copy(v[l][a][:], tab[a][:].indirect(lists[l][:]))
             if a == 0:
-                load_w1(1)
+                load_w1(w1_last, slice(KP - 1, KP), 0)
+                load_w1(w1_upper, slice(0, KP), 1)
                 nc.sync.dma_start(out=w2_raw[:], in_=w2.rearrange("(b p t) n -> p b t n", b=HP, t=4))
 
         f = {}
@@ -121,7 +122,7 @@ def tile_list_peer_clock_disagreement_kernel(
                     out=f[(u, l)][:],
                     lhsT=v[l][a][:, P * jb : P * (jb + 1)].bitcast(FP8X4),
                     lhsT_scale=v_sc[:, a, c0 : c0 + P],
-                    rhs=w1[b][:, a, :].bitcast(FP4X4),
+                    rhs=w1[b][a].bitcast(FP4X4),
                     rhs_scale=w1_sc[:, a, PASS * b : PASS * (b + 1)],
                     start=(a == 0),
                     stop=(a == KP - 1),
@@ -191,20 +192,23 @@ def tile_list_peer_clock_disagreement_kernel(
 
         acc = {}
 
+        def score_pass(target, jb, b, m, start, stop):
+            cols = slice(P * m, P * (m + 1))
+            nc.tensor.matmul_mx(
+                out=target,
+                lhsT=w2_q[b][:, cols].bitcast(FP8X4),
+                lhsT_scale=w2_sc[b][:, cols],
+                rhs=h_q[(jb, b)].bitcast(FP8X4),
+                rhs_scale=h_sc[(jb, b)],
+                start=start,
+                stop=stop,
+            )
+
         def score_passes(jb, b):
             if b == 0:
                 acc[jb] = psum.tile([P, NB, P], F32, name="acc", tag="f0", bufs=2)
             for m in range(NB):
-                cols = slice(P * m, P * (m + 1))
-                nc.tensor.matmul_mx(
-                    out=acc[jb][:, m, :],
-                    lhsT=w2_q[b][:, cols].bitcast(FP8X4),
-                    lhsT_scale=w2_sc[b][:, cols],
-                    rhs=h_q[(jb, b)].bitcast(FP8X4),
-                    rhs_scale=h_sc[(jb, b)],
-                    start=(b == 0 and m == 0),
-                    stop=(b == HP - 1 and m == NB - 1),
-                )
+                score_pass(acc[jb][:, m, :], jb, b, m, b == 0 and m == 0, b == HP - 1 and m == NB - 1)
 
         def store(jb):
             result = ring.tile([P, NB, P], F32, name="result", tag="result", bufs=2)
@@ -228,10 +232,11 @@ def tile_list_peer_clock_disagreement_kernel(
         for l in range(1, LISTS):
             for u in range(2):
                 product(u, l, [KP - 1])
-            product(l + 1, 0, range(KP))
-            copy_first(l + 1)
 
         for u in range(UNITS):
+            if u + 2 < UNITS and u + 2 not in EARLY:
+                product(u + 2, 0, range(KP))
+                copy_first(u + 2)
             extremes_of_two(u)
             if u in (2, 4, 6):
                 turn((u - 2, u - 1))
@@ -247,9 +252,6 @@ def tile_list_peer_clock_disagreement_kernel(
             spread(u)
             if u + 2 < UNITS:
                 product(u + 2, 2, range(KP))
-            if u < 2:
-                product(5 + 2 * u, 0, range(KP))
-                copy_first(5 + 2 * u)
             if u in (0, 2):
                 for m in range(NB):
                     round_w2(NB * (u // 2) + m)
@@ -260,7 +262,16 @@ def tile_list_peer_clock_disagreement_kernel(
         quantise_h((4, 5))
         quantise_h((6,))
         scores(2)
-        score_passes(3, 0)
+        last = [psum.tile([P, P], F32, name="last", tag=("f1", "f1", "f2")[m], bufs=2) for m in range(NB)]
+        for m in range(NB):
+            score_pass(last[m][:], JB - 1, 0, m, True, False)
         quantise_h((7,))
-        score_passes(3, 1)
-        store(3)
+        for m in range(NB):
+            score_pass(last[m][:], JB - 1, 1, m, False, True)
+            piece = keep.tile([P, P], F32, name="piece%d" % m)
+            if m == 1:
+                nc.vector.tensor_copy(piece[:], last[m][:])
+            else:
+                nc.scalar.copy(out=piece[:], in_=last[m][:])
+            queue = nc.scalar if m == 2 else nc.sync
+            queue.dma_start(out=out[P * m : P * (m + 1), P * (JB - 1) : P * JB], in_=piece[:])

@@ -29,6 +29,7 @@ UNITS = HP * JB
 ROW0 = P - 16 * KP
 ORDER = [(0, 0), (1, 0), (0, 1), (1, 1), (2, 0), (2, 1), (3, 0), (3, 1)]
 EARLY = (4, 6)
+TAB0 = 4 * T * (KP - 1)
 
 
 def tile_list_peer_clock_disagreement_kernel(
@@ -42,21 +43,21 @@ def tile_list_peer_clock_disagreement_kernel(
         psum = ctx.enter_context(tc.psum_pool(name="psum", bufs=1))
 
         lists = [keep.tile([P, S // 16], U16, name="list%d" % l) for l in range(LISTS)]
-        tab = [reuse.tile([P, T], U32, name="tab%d" % a, align_bytes=64, offset=4 * T * a) for a in range(KP)]
-        tab_sc = reuse.tile([P, T], U8, name="tab_sc", align_bytes=64, offset=4 * T * (KP - 1))
+        tab = [reuse.tile([P, T], U32, name="tab%d" % a, align_bytes=64, offset=4 * T * (KP - 1 - a)) for a in range(KP)]
+        tab_sc = reuse.tile([P, T], U8, name="tab_sc", align_bytes=64, offset=0)
         picked_sc = keep.tile([P, LISTS * S], U8, name="picked_sc", align_bytes=64)
         v_sc = keep.tile([P, KP, LISTS * S], U8, name="v_sc", align_bytes=64)
         v = [[keep.tile([P, S], U32, name="v%d_%d" % (l, a), align_bytes=64) for a in range(KP)] for l in range(LISTS)]
         w1_early = keep.tile([P, KP - 1, 2 * PASS], U8, name="w1_early", align_bytes=64)
-        w1_last = reuse.tile([P, 1, 2 * PASS], U8, name="w1_last", align_bytes=64, offset=0)
-        w1_upper = reuse.tile([P, KP, 2 * PASS], U8, name="w1_upper", align_bytes=64, offset=2 * PASS)
+        w1_last = reuse.tile([P, 1, 2 * PASS], U8, name="w1_last", align_bytes=64, offset=TAB0 + 4 * P)
+        w1_upper = reuse.tile([P, KP, 2 * PASS], U8, name="w1_upper", align_bytes=64, offset=TAB0 + 4 * P + 2 * PASS)
         w1 = [[w1_early[:, 0, :], w1_early[:, 1, :], w1_last[:, 0, :]], [w1_upper[:, a, :] for a in range(KP)]]
         w1_sc = keep.tile([P, KP, H], U8, name="w1_sc", align_bytes=64)
-        w2_raw = reuse.tile([P, HP, 4, N], F32, name="w2_raw", align_bytes=64, offset=T)
+        w2_raw = reuse.tile([P, HP, 4, N], F32, name="w2_raw", align_bytes=64, offset=TAB0 + 4 * P + 8 * PASS)
         w2_bf = [keep.tile([P, N, 4], BF16, name="w2_bf%d" % b, align_bytes=64) for b in range(HP)]
         w2_q = [keep.tile([P, N], U32, name="w2_q%d" % b, align_bytes=64) for b in range(HP)]
         w2_sc = [keep.tile([P, N], U8, name="w2_sc%d" % b, align_bytes=64) for b in range(HP)]
-        ident = keep.tile([P, P], F32, name="ident", align_bytes=64)
+        ident = reuse.tile([P, P], F32, name="ident", align_bytes=64, offset=TAB0)
 
         def load_tab(a):
             nc.sync.dma_start(out=tab[a][:].bitcast(I32), in_=tab_words[a].rearrange("p t i -> p (t i)").bitcast(I32))
@@ -72,14 +73,12 @@ def tile_list_peer_clock_disagreement_kernel(
         load_tab(0)
         load_w1(w1_early, slice(0, KP - 1), 0)
         load_tab(1)
-        nc.vector.memset(tab_sc[0:64, :].bitcast(I32), 0)
-        nc.vector.memset(tab_sc[64:ROW0, :].bitcast(I32), 0)
+        nc.vector.memset(tab_sc[0:ROW0, :].bitcast(I32), 0)
         nc.vector.memset(v_sc[:].bitcast(I32), 0)
         nc.gpsimd.memset(w1_sc[:].bitcast(I32), 0)
         for q in range(4):
             rows = w1_scales[:, 4 * q : 4 * q + 4, :].rearrange("a r n -> r a n")
             nc.gpsimd.dma_start(out=w1_sc[32 * q : 32 * q + 4].bitcast(I32), in_=rows.bitcast(I32))
-        make_identity(nc, ident[:])
 
         for l in range(LISTS):
             nc.vector.tensor_copy(picked_sc[:, S * l : S * (l + 1)], tab_sc[:].indirect(lists[l][:]))
@@ -98,6 +97,8 @@ def tile_list_peer_clock_disagreement_kernel(
                 load_w1(w1_last, slice(KP - 1, KP), 0)
                 load_w1(w1_upper, slice(0, KP), 1)
                 nc.sync.dma_start(out=w2_raw[:], in_=w2.rearrange("(b p t) n -> p b t n", b=HP, t=4))
+
+        make_identity(nc, ident[:])
 
         f = {}
         first_copy = {}
@@ -141,16 +142,16 @@ def tile_list_peer_clock_disagreement_kernel(
         def extremes_of_two(u):
             high[u] = ring.tile([P, PASS], F32, name="high2", tag="high2", bufs=2)
             low[u] = ring.tile([P, PASS], F32, name="low2", tag="low2", bufs=2)
-            nc.vector.tensor_tensor(flat(high[u]), dealt(u, 1), flat(first_copy[u]), MAX)
-            nc.vector.tensor_tensor(flat(low[u]), dealt(u, 1), flat(first_copy[u]), MIN)
+            nc.vector.tensor_tensor(flat(high[u]), flat(first_copy[u]), dealt(u, 1), MAX)
+            nc.vector.tensor_tensor(flat(low[u]), flat(first_copy[u]), dealt(u, 1), MIN)
 
         def third_high(u):
             high3[u] = ring.tile([P, PASS], F32, name="high3", tag="high3", bufs=2)
-            nc.vector.tensor_tensor(flat(high3[u]), dealt(u, 2), flat(high[u]), MAX)
+            nc.vector.tensor_tensor(flat(high3[u]), flat(high[u]), dealt(u, 2), MAX)
 
         def spread(u):
             low3 = ring.tile([P, PASS], F32, name="low3", tag="low3", bufs=2)
-            nc.vector.tensor_tensor(flat(low3), dealt(u, 2), flat(low[u]), MIN)
+            nc.vector.tensor_tensor(flat(low3), flat(low[u]), dealt(u, 2), MIN)
             h_t[u] = ring.tile([P, PASS], BF16, name="h_t", tag="h_t", bufs=3, align_bytes=64)
             engine = nc.vector if u == UNITS - 1 else nc.gpsimd
             engine.tensor_tensor(h_t[u][:], high3[u][:], low3[:], SUB)

from contextlib import ExitStack

import concourse.mybir as mybir
from concourse.masks import make_identity

K, T, S, H, N = 1536, 4096, 512, 1024, 384
FLOPS = 2 * (3 * K * H * S + H * N * S)

F32 = mybir.dt.float32
BF16 = mybir.dt.bfloat16
I32 = mybir.dt.int32
U32 = mybir.dt.uint32
U16 = mybir.dt.uint16
U8 = mybir.dt.uint8
FP8X4 = mybir.dt.float8_e4m3fn_x4
FP4X4 = mybir.dt.float4_e2m1fn_x4
MAX = mybir.AluOpType.max
MIN = mybir.AluOpType.min
SUB = mybir.AluOpType.subtract

P = 128
PASS = 512
KP = K // PASS
HP = H // PASS
LISTS = 3
JB = S // P
NB = N // P
UNITS = HP * JB
ROW0 = P - 16 * KP
ORDER = [(0, 0), (1, 0), (0, 1), (1, 1), (2, 0), (2, 1), (3, 0), (3, 1)]
EARLY = (4, 6)
TAB0 = 4 * T * (KP - 1)


def tile_list_peer_clock_disagreement_kernel(
    tc, tab_words, tab_scales, w1_words, w1_scales, w2, offs, offs2, offs3, out
):
    nc = tc.nc
    with ExitStack() as ctx:
        keep = ctx.enter_context(tc.tile_pool(name="keep", bufs=1))
        ring = ctx.enter_context(tc.tile_pool(name="ring", bufs=3))
        reuse = ctx.enter_context(tc.tile_pool(name="reuse", bufs=1))
        psum = ctx.enter_context(tc.psum_pool(name="psum", bufs=1))

        lists = [keep.tile([P, S // 16], U16, name="list%d" % l) for l in range(LISTS)]
        tab = [reuse.tile([P, T], U32, name="tab%d" % a, align_bytes=64, offset=4 * T * (KP - 1 - a)) for a in range(KP)]
        tab_sc = reuse.tile([P, T], U8, name="tab_sc", align_bytes=64, offset=0)
        picked_sc = keep.tile([P, LISTS * S], U8, name="picked_sc", align_bytes=64)
        v_sc = keep.tile([P, KP, LISTS * S], U8, name="v_sc", align_bytes=64)
        v = [[keep.tile([P, S], U32, name="v%d_%d" % (l, a), align_bytes=64) for a in range(KP)] for l in range(LISTS)]
        w1_early = keep.tile([P, KP - 1, 2 * PASS], U8, name="w1_early", align_bytes=64)
        w1_last = reuse.tile([P, 1, 2 * PASS], U8, name="w1_last", align_bytes=64, offset=TAB0 + 4 * P)
        w1_upper = reuse.tile([P, KP, 2 * PASS], U8, name="w1_upper", align_bytes=64, offset=TAB0 + 4 * P + 2 * PASS)
        w1 = [[w1_early[:, 0, :], w1_early[:, 1, :], w1_last[:, 0, :]], [w1_upper[:, a, :] for a in range(KP)]]
        w1_sc = keep.tile([P, KP, H], U8, name="w1_sc", align_bytes=64)
        w2_raw = reuse.tile([P, HP, 4, N], F32, name="w2_raw", align_bytes=64, offset=TAB0 + 4 * P + 8 * PASS)
        w2_bf = [keep.tile([P, N, 4], BF16, name="w2_bf%d" % b, align_bytes=64) for b in range(HP)]
        w2_q = [keep.tile([P, N], U32, name="w2_q%d" % b, align_bytes=64) for b in range(HP)]
        w2_sc = [keep.tile([P, N], U8, name="w2_sc%d" % b, align_bytes=64) for b in range(HP)]
        ident = reuse.tile([P, P], F32, name="ident", align_bytes=64, offset=TAB0)

        def load_tab(a):
            nc.sync.dma_start(out=tab[a][:].bitcast(I32), in_=tab_words[a].rearrange("p t i -> p (t i)").bitcast(I32))

        def load_w1(tile, passes, b):
            cols = w1_words[passes, :, 2 * PASS * b : 2 * PASS * (b + 1)]
            nc.sync.dma_start(out=tile[:].bitcast(I32), in_=cols.rearrange("a p n -> p a n").bitcast(I32))

        for a in range(KP):
            nc.scalar.dma_start(out=tab_sc[ROW0 + a : P : KP, :].bitcast(I32), in_=tab_scales[a].bitcast(I32))
        for tile, src in zip(lists, (offs, offs2, offs3)):
            nc.sync.dma_start(tile[:], src)
        load_tab(0)
        load_w1(w1_early, slice(0, KP - 1), 0)
        load_tab(1)
        nc.vector.memset(tab_sc[0:ROW0, :].bitcast(I32), 0)
        nc.vector.memset(v_sc[:].bitcast(I32), 0)
        nc.gpsimd.memset(w1_sc[:].bitcast(I32), 0)
        for q in range(4):
            rows = w1_scales[:, 4 * q : 4 * q + 4, :].rearrange("a r n -> r a n")
            nc.gpsimd.dma_start(out=w1_sc[32 * q : 32 * q + 4].bitcast(I32), in_=rows.bitcast(I32))

        for l in range(LISTS):
            nc.vector.tensor_copy(picked_sc[:, S * l : S * (l + 1)], tab_sc[:].indirect(lists[l][:]))
        for q in range(4):
            first = ROW0 + 4 * KP * q
            queue = nc.sync if q % 2 == 0 else nc.scalar
            queue.dma_start(
                out=v_sc[32 * q : 32 * q + 4].bitcast(I32),
                in_=picked_sc[first : first + 4 * KP, :].bitcast(I32),
            )
        load_tab(2)
        for a in range(KP):
            for l in range(LISTS):
                nc.vector.tensor_copy(v[l][a][:], tab[a][:].indirect(lists[l][:]))
            if a == 0:
                load_w1(w1_last, slice(KP - 1, KP), 0)
                load_w1(w1_upper, slice(0, KP), 1)
                nc.sync.dma_start(out=w2_raw[:], in_=w2.rearrange("(b p t) n -> p b t n", b=HP, t=4))

        make_identity(nc, ident[:])

        f = {}
        first_copy = {}
        high = {}
        low = {}
        high3 = {}
        h_q = {}
        h_sc = {}
        h_t = {}
        h_bf = {}

        def product(u, l, passes):
            jb, b = ORDER[u]
            if (u, l) not in f:
                if l == 0 and u in EARLY:
                    f[(u, l)] = psum.tile([P, PASS], F32, name="f_early", tag=("turned", "acc")[EARLY.index(u)])
                else:
                    f[(u, l)] = psum.tile([P, PASS], F32, name="f%d" % l, tag="f%d" % l, bufs=2)
            for a in passes:
                c0 = S * l + P * jb
                nc.tensor.matmul_mx(
                    out=f[(u, l)][:],
                    lhsT=v[l][a][:, P * jb : P * (jb + 1)].bitcast(FP8X4),
                    lhsT_scale=v_sc[:, a, c0 : c0 + P],
                    rhs=w1[b][a].bitcast(FP4X4),
                    rhs_scale=w1_sc[:, a, PASS * b : PASS * (b + 1)],
                    start=(a == 0),
                    stop=(a == KP - 1),
                )

        def dealt(u, l):
            return f[(u, l)][:].rearrange("j (q u e) -> j u q e", u=2, e=2)

        def flat(t):
            return t[:].rearrange("j (u q e) -> j u q e", u=2, e=2)

        def copy_first(u):
            first_copy[u] = ring.tile([P, PASS], F32, name="first_copy", tag="first_copy", bufs=UNITS)
            nc.scalar.copy(out=flat(first_copy[u]), in_=dealt(u, 0))

        def extremes_of_two(u):
            high[u] = ring.tile([P, PASS], F32, name="high2", tag="high2", bufs=2)
            low[u] = ring.tile([P, PASS], F32, name="low2", tag="low2", bufs=2)
            nc.vector.tensor_tensor(flat(high[u]), flat(first_copy[u]), dealt(u, 1), MAX)
            nc.vector.tensor_tensor(flat(low[u]), flat(first_copy[u]), dealt(u, 1), MIN)

        def third_high(u):
            high3[u] = ring.tile([P, PASS], F32, name="high3", tag="high3", bufs=2)
            nc.vector.tensor_tensor(flat(high3[u]), flat(high[u]), dealt(u, 2), MAX)

        def spread(u):
            low3 = ring.tile([P, PASS], F32, name="low3", tag="low3", bufs=2)
            nc.vector.tensor_tensor(flat(low3), flat(low[u]), dealt(u, 2), MIN)
            h_t[u] = ring.tile([P, PASS], BF16, name="h_t", tag="h_t", bufs=3, align_bytes=64)
            engine = nc.vector if u == UNITS - 1 else nc.gpsimd
            engine.tensor_tensor(h_t[u][:], high3[u][:], low3[:], SUB)

        def turn(units):
            n = len(units)
            turned = psum.tile([P, n, 2, P], F32, name="turned", tag="turned")
            for k, u in enumerate(units):
                words = h_t[u][:].bitcast(F32)
                for half in range(2):
                    nc.tensor.transpose(turned[:, k, half, :], words[:, P * half : P * (half + 1)], ident[:])
            h_bf[units] = ring.tile([P, n * 4 * P], BF16, name="h_bf", tag="h_bf", bufs=3, align_bytes=64)
            nc.scalar.copy(
                out=h_bf[units][:].bitcast(F32).rearrange("q (k j u) -> q k j u", k=n, u=2),
                in_=turned[:].rearrange("q k u j -> q k j u"),
            )

        def quantise_h(units):
            n = len(units)
            codes = keep.tile([P, n * P], U32, name="h_q%d" % units[0], align_bytes=64)
            scales = keep.tile([P, n * P], U8, name="h_sc%d" % units[0], align_bytes=64)
            nc.vector.quantize_mx(out=codes[:].bitcast(FP8X4), scales=scales[:], in_=h_bf[units][:])
            for k, u in enumerate(units):
                h_q[ORDER[u]] = codes[:, P * k : P * (k + 1)]
                h_sc[ORDER[u]] = scales[:, P * k : P * (k + 1)]

        def round_w2(piece):
            b, m = divmod(piece, NB)
            cols = slice(P * m, P * (m + 1))
            nc.scalar.copy(
                out=w2_bf[b][:, cols, :],
                in_=w2_raw[:, b, :, cols].rearrange("p t n -> p n t"),
            )

        def quantise_w2(b):
            nc.vector.quantize_mx(
                out=w2_q[b][:].bitcast(FP8X4), scales=w2_sc[b][:], in_=w2_bf[b][:].rearrange("p n t -> p (n t)")
            )

        acc = {}

        def score_pass(target, jb, b, m, start, stop):
            cols = slice(P * m, P * (m + 1))
            nc.tensor.matmul_mx(
                out=target,
                lhsT=w2_q[b][:, cols].bitcast(FP8X4),
                lhsT_scale=w2_sc[b][:, cols],
                rhs=h_q[(jb, b)].bitcast(FP8X4),
                rhs_scale=h_sc[(jb, b)],
                start=start,
                stop=stop,
            )

        def score_passes(jb, b):
            if b == 0:
                acc[jb] = psum.tile([P, NB, P], F32, name="acc", tag="f0", bufs=2)
            for m in range(NB):
                score_pass(acc[jb][:, m, :], jb, b, m, b == 0 and m == 0, b == HP - 1 and m == NB - 1)

        def store(jb):
            result = ring.tile([P, NB, P], F32, name="result", tag="result", bufs=2)
            nc.scalar.copy(out=result[:], in_=acc[jb][:])
            nc.sync.dma_start(
                out=out.rearrange("(m p) j -> p m j", p=P)[:, :, P * jb : P * (jb + 1)], in_=result[:]
            )

        def scores(jb):
            for b in range(HP):
                score_passes(jb, b)
            store(jb)

        for a in range(KP - 1):
            for l in range(LISTS):
                for u in (0, 1) + (EARLY if l == 0 else ()):
                    product(u, l, [a])
        for u in (0, 1) + EARLY:
            product(u, 0, [KP - 1])
            copy_first(u)
        for l in range(1, LISTS):
            for u in range(2):
                product(u, l, [KP - 1])

        for u in range(UNITS):
            if u + 2 < UNITS and u + 2 not in EARLY:
                product(u + 2, 0, range(KP))
                copy_first(u + 2)
            extremes_of_two(u)
            if u in (2, 4, 6):
                turn((u - 2, u - 1))
            if u == UNITS - 1:
                turn((u - 1,))
            if u + 2 < UNITS:
                product(u + 2, 1, range(KP))
            third_high(u)
            if u in (2, 4):
                quantise_w2(u // 2 - 1)
            if u in (3, 5):
                quantise_h((u - 3, u - 2))
            spread(u)
            if u + 2 < UNITS:
                product(u + 2, 2, range(KP))
            if u in (0, 2):
                for m in range(NB):
                    round_w2(NB * (u // 2) + m)
            if u == 5:
                scores(0)
                scores(1)
        turn((7,))
        quantise_h((4, 5))
        quantise_h((6,))
        scores(2)
        last = [psum.tile([P, P], F32, name="last", tag=("f1", "f1", "f2")[m], bufs=2) for m in range(NB)]
        for m in range(NB):
            score_pass(last[m][:], JB - 1, 0, m, True, False)
        quantise_h((7,))
        for m in range(NB):
            score_pass(last[m][:], JB - 1, 1, m, False, True)
            piece = keep.tile([P, P], F32, name="piece%d" % m)
            if m == 1:
                nc.vector.tensor_copy(piece[:], last[m][:])
            else:
                nc.scalar.copy(out=piece[:], in_=last[m][:])
            queue = nc.scalar if m == 2 else nc.sync
            queue.dma_start(out=out[P * m : P * (m + 1), P * (JB - 1) : P * JB], in_=piece[:])
